import numpy as np, ml_dtypes
CORES = [3,5,19,21,35,37,51,53,67,69]
N = 10
import mx_ref
NC, GR, GC, KT = 128, 5, 2, 4
TS = GC * KT
CH = GR * NC // GC
BF = ml_dtypes.bfloat16
def setup_inputs(rng):
    def f(*shape):
        return mx_ref.flush((rng.standard_normal(shape, dtype=np.float32) * np.exp2(rng.integers(-2, 3, shape[:-1] + (1,)))).astype(BF))
    return {"w": f(N, 128, KT * 512), "x": f(N, 128, KT * 4 * NC)}
def setup_inputs_blocks(rng):
    d = setup_inputs(rng)
    for k in ("w", "x"): d[k] = mx_ref.spread(d[k], rng, 2)
    return d
def setup_inputs_wide(rng):
    d = setup_inputs(rng)
    for k in ("w", "x"): d[k] = mx_ref.flush((d[k].astype(np.float32) * np.exp2(rng.integers(-8, 9, (N, 1, 1))).astype(np.float32)).astype(BF))
    return d
def setup_inputs_zeros(rng):
    d = setup_inputs(rng); v = d["x"].reshape(N, 128, -1, 4).copy()
    v[np.broadcast_to((rng.random((N, 1, v.shape[2], 1)) < 0.33), v.shape)] = 0
    d["x"] = v.reshape(d["x"].shape)
    return d
def reference(w, x):
    QX = [[mx_ref.quantize(x[r][:, 4 * NC * t:4 * NC * t + 4 * NC]) for t in range(KT)] for r in range(N)]
    y = np.zeros((N, 128, CH), np.float32)
    for i in range(GR):
        for s in range(TS):
            k, t = s // KT, s % KT
            qw = mx_ref.quantize(w[i * GC + k][:, 512 * t:512 * t + 512])
            p = np.concatenate([mx_ref.matmul(qw, QX[g * GC + k][t]) for g in range(GR)], axis=1)
            Y = p if s == 0 else Y + p
        for c in range(GC):
            y[i * GC + c] = Y[:, CH * c:CH * c + CH]
    return {"y": y}

@@ -1,0 +1,262 @@
+from concourse.bass import DstId, RemoteDMATransfer
+from concourse.mybir import dt
+
+N, GR, GC, KT, NC, CH = 10, 5, 2, 4, 128, 320
+XH0, XH1, XO, WO, WP, XF = 0, 256, 512, 1024, 1536, 2048
+QCOLS = XF + 4 * 512
+NO, NE = 0, 0
+
+SCRATCH = {
+    "xb": ("sbuf", [128, 2048], "bfloat16"),
+    "wb": ("sbuf", [128, 2048], "bfloat16"),
+    "q": ("sbuf", [128, QCOLS], "float8_e4m3fn_x4"),
+    "p": ("sbuf", [128, QCOLS], "uint8"),
+    "ob": ("sbuf", [128, CH], "float32"),
+    "ps": ("psum", [128, 3 * 512], "float32"),
+}
+SEMAPHORES = (["lx0", "lx1", "lw0", "lw1", "qx0", "qx1", "qw0", "qw1", "aw", "sent", "rl", "f0", "f1"]
+              + ["%s%d" % (n, j) for n in "aeo" for j in range(6)]
+              + ["%s%d" % (n, b) for n in ("mm", "cp", "st") for b in range(3)])
+MEMO = {}
+
+
+def blocks(c):
+    out = []
+    for g in range(GR):
+        lo, hi = max(NC * g, CH * c), min(NC * g + NC, CH * c + CH)
+        if hi > lo:
+            out.append((g, lo - NC * g, hi - lo))
+    return out
+
+
+def seg_src(g, k):
+    segs = [(c, off, w) for c in range(GC) for (gg, off, w) in blocks(c) if gg == g]
+    segs.sort(key=lambda s: s[0] != k)
+    out, col = [], XO
+    for (c, off, w) in segs:
+        out.append((c, off, w, col))
+        col += KT * w
+    return out
+
+
+def slot(i, c, g, kk):
+    if (i, c) == (g, kk):
+        return XO, None
+    full = [b[0] for b in blocks(c) if b[2] == NC]
+    if g in full:
+        j = 2 * full.index(g) + kk
+        return XF + 512 * j, "a%d" % (2 + j)
+    if i == g or kk == 1:
+        return XH1, "a1"
+    return XH0, "a0"
+
+
+def row_at(g, k, r):
+    return (g + r) % GR if k == 0 else (g - r) % GR
+
+
+def bits(m):
+    return [b for b in range(m.bit_length()) if (m >> b) & 1]
+
+
+def lane_of(t):
+    return "o" if t < NO else "e" if t < NO + NE else "a"
+
+
+def plan_all(cores, topo):
+    calls = {}
+    every = range(topo.CHIPS * topo.CORES_PER_CHIP)
+
+    def add(core, order, waits, pool, trs):
+        calls.setdefault(core, []).append((order, waits, pool, trs))
+
+    def on(ch):
+        return [c for c in every if topo.chip(c) == ch]
+
+    def mate_of(ch):
+        return [m for m in range(topo.CHIPS) if topo.mates(ch, m)][0]
+
+    lanes = {"o": (0, NO), "e": (NO, NE), "a": (NO + NE, KT - NO - NE)}
+    for s in range(N):
+        g, k = divmod(s, GC)
+        me, mate = cores[s], cores[g * GC + (1 - k)]
+        lo = bits(topo.mask(me, cores[row_at(g, k, 1) * GC + k]))
+        hi = [b for b in bits(topo.mask(me, mate)) if b not in lo]
+        S = seg_src(g, k)
+        free = [c for c in on(topo.chip(me)) if topo.die(c) == topo.die(me) and c not in cores]
+        port = [c for c in free if topo.may_write(c, on(mate_of(topo.chip(me)))[0])]
+        relay = {"o": port[0], "e": [c for c in free if c != port[0]][0]}
+
+        def far(lane, r, base=None):
+            i, (t0, n), out = row_at(g, k, r), lanes[lane], []
+            for (c, off, w, sc) in S:
+                dc, sn = slot(i, c, g, k)
+                out.append(("q", sc + w * t0 if base is None else base, w * n, cores[i * GC + c], (dc + w * t0, lane + sn[1:])))
+                if base is not None:
+                    base += w * n
+            return out
+
+        def planes(r):
+            i = row_at(g, k, r)
+            return [("p", sc, KT * w, cores[i * GC + c], slot(i, c, g, k)) for (c, off, w, sc) in S]
+
+        for lane in ("o", "e"):
+            t0, n = lanes[lane]
+            if n:
+                trs, rc = [], 0
+                for (c, off, w, sc) in S:
+                    trs.append(("q", sc + w * t0, w * n, relay[lane], (rc, "rl")))
+                    rc += w * n
+                add(me, 0, ["x"], hi, trs)
+                for r in range(1, GR):
+                    R, dest = relay[lane], cores[row_at(g, k, r) * GC + k]
+                    if lane == "e":
+                        add(R, r, ["rl"], bits(topo.mask(R, dest)), far("e", r, 0))
+                    else:
+                        F = [c for c in on(mate_of(topo.chip(dest))) if topo.die(c) == topo.die(R) and topo.may_write(c, dest)]
+                        f, j = F[(r - 1) % len(F)], (r - 1) // len(F)
+                        add(R, r, ["rl"], bits(topo.mask(R, f)), [("q", 0, rc, f, (rc * j, "f%d" % j))])
+                        add(f, r, ["f%d" % j], bits(topo.mask(f, dest)), far("o", r, rc * j))
+        add(me, 1, ["x"], lo, far("a", 1))
+        add(me, 2, ["x"], lo, [t for r in range(1, GR) for t in planes(r)])
+        add(me, 3, ["x"], lo, far("a", 2))
+        for buf in ("q", "p"):
+            tx = [(buf, sc, KT * w, mate, slot(g, c, g, k)) for (c, off, w, sc) in S if c != k]
+            tw = [(buf, WO, 512, mate, (WP, "aw"))]
+            if tx and tx[0][2] == 512:
+                add(me, 4, ["w"], hi, tx + tw)
+            else:
+                if tx:
+                    add(me, 4, ["x"], hi, tx)
+                add(me, 4, ["w"], hi, tw)
+        add(me, 5, ["x"], lo, far("a", 3))
+        add(me, 6, ["x"], lo, far("a", 4))
+    need = {}
+    for c in calls:
+        calls[c].sort(key=lambda x: x[0])
+        for (_, _, pool, trs) in calls[c]:
+            for t in trs:
+                d = need.setdefault(t[3], {})
+                d[t[4][1]] = d.get(t[4][1], 0) + len(pool) // len(trs)
+    return calls, need
+
+
+def send_all(g, T, topo, calls, need):
+    sem = T.sem
+    waited, sent = set(), 0
+    for (_, waits, pool, trs) in calls:
+        for key in waits:
+            if key not in waited:
+                waited.add(key)
+                if key in ("x", "w"):
+                    for h in range(2):
+                        g.wait_ge(sem["q%s%d" % (key, h)], 1)
+                else:
+                    g.wait_ge(sem[key], need[key])
+        n = len(pool) // len(trs)
+        out = []
+        for j, (buf, sc, nc, d, (dc, sn)) in enumerate(trs):
+            mask = sum(1 << b for b in pool[j * n:(j + 1) * n])
+            if buf == "q":
+                src, dst = T.q[:, sc:sc + nc].bitcast(dt.uint8), T.q[:, dc:dc + nc].bitcast(dt.uint8)
+            else:
+                src, dst = T.p[:, sc:sc + nc], T.p[:, dc:dc + nc]
+            rid, pid, _ = topo.addr(d)
+            out.append((src, dst, rid, pid, mask, sem[sn]))
+            sent += n
+        if len(out) == 1:
+            src, dst, rid, pid, mask, sn = out[0]
+            g.remote_dma(out_ap=dst, in_ap=src, remote_sem=sn, local_sem=sem.sent, pid=pid, routing_id=rid, dma_engine_mask=mask)
+        else:
+            g.remote_dma_fused([RemoteDMATransfer(dst_ids=[DstId(rid=rid, pnc=pid)], dma_engine_mask=mask, remote_sem=sn, src=src, dst=dst)
+                                for (src, dst, rid, pid, mask, sn) in out], local_sem=sem.sent)
+    g.wait_ge(sem.sent, sent)
+
+
+def rank_program(g, core, T, topo):
+    cores = list(T.cores)
+    if "plan" not in MEMO:
+        MEMO["plan"] = plan_all(cores, topo)
+    calls, needs = MEMO["plan"]
+    need = needs.get(core, {})
+    r = T.rank_of(core)
+    if r is None:
+        if core in calls:
+            send_all(g, T, topo, calls[core], need)
+        return
+    i, k = divmod(r, GC)
+    sem = T.sem
+
+    dq = [g.sync, g.scalar]
+    S = seg_src(i, k)
+    if len(S) == 1:
+        for h in range(2):
+            dq[h].dma_start(T.xb[:, 1024 * h:1024 * h + 1024], T.x[:, 1024 * h:1024 * h + 1024]).then_inc(sem["lx%d" % h], 16)
+        nl = 16
+    else:
+        for j, (c, off, w, sc) in enumerate(S):
+            for t in range(KT):
+                a = 4 * (sc - XO) + 4 * w * t
+                dq[t // 2].dma_start(T.xb[:, a:a + 4 * w], T.x[:, 512 * t + 4 * off:512 * t + 4 * off + 4 * w]).then_inc(sem["lx%d" % j], 16)
+        nl = 16 * KT
+    for h in range(2):
+        dq[h].dma_start(T.wb[:, 1024 * h:1024 * h + 1024], T.w[:, 1024 * h:1024 * h + 1024]).then_inc(sem["lw%d" % h], 16)
+
+    v = g.vector
+    for (nm, buf, col, cnt) in (("x", T.xb, XO, nl), ("w", T.wb, WO, 16)):
+        for h in range(2):
+            v.wait_ge(sem["l%s%d" % (nm, h)], cnt)
+            a = col + 256 * h
+            v.quantize_mx(T.q[:, a:a + 256], T.p[:, a:a + 256], buf[:, 1024 * h:1024 * h + 1024]).then_inc(sem["q%s%d" % (nm, h)], 1)
+
+    send_all(g, T, topo, calls[core], need)
+
+    def due(lane, gg, kk):
+        st = [row_at(gg, kk, q) for q in range(GR)].index(i)
+        return {"a": 1 + st * (KT - NO - NE), "e": 5 + st * NE, "o": 9 + (st + 1) * NO}[lane]
+
+    ops = []
+    for b, (gg, off, w) in enumerate(blocks(k)):
+        for kk in range(GC):
+            col, sn = slot(i, k, gg, kk)
+            for t in range(KT):
+                deps, est = [sn], 0 if sn is None else 1
+                if gg != i:
+                    deps.append(lane_of(t) + sn[1:])
+                    est = max(due("a", gg, kk), due(lane_of(t), gg, kk))
+                if kk != k:
+                    deps.append("aw")
+                    est = max(est, 1)
+                if w < NC and t == KT - 1 and col == XH0:
+                    deps += ["a1", lane_of(0) + "1"]
+                    est = max(est, due("a", gg, 1), due(lane_of(0), gg, 1))
+                ops.append((est, b, kk, t, col + w * t, deps))
+    ops.sort(key=lambda o: o[:4])
+    te = g.tensor
+    for nm in ("qx0", "qx1", "qw0", "qw1"):
+        te.wait_ge(sem[nm], 1)
+    seen, done = set(), []
+    for n, (est, b, kk, t, col, deps) in enumerate(ops):
+        for sn in deps:
+            if sn is not None and sn not in seen:
+                seen.add(sn)
+                te.wait_ge(sem[sn], need[sn])
+        first = not any(o[1] == b for o in ops[:n])
+        last = not any(o[1] == b for o in ops[n + 1:])
+        wc = (WO if kk == k else WP) + NC * t
+        ins = te.matmul_mx(T.ps[:, 512 * b:512 * b + NC], T.q[:, wc:wc + NC], T.p[:, wc:wc + NC],
+                           T.q[:, col:col + NC], T.p[:, col:col + NC], first, last)
+        if last:
+            ins.then_inc(sem["mm%d" % b], 1)
+            done.append(b)
+
+    for n, b in enumerate(done):
+        gg, off, w = blocks(k)[b]
+        y0 = NC * gg + off - CH * k
+        v.wait_ge(sem["mm%d" % b], 1)
+        v.tensor_copy(T.ob[:, y0:y0 + w], T.ps[:, 512 * b:512 * b + w]).then_inc(sem["cp%d" % b], 1)
+        d = dq[n % 2]
+        d.wait_ge(sem["cp%d" % b], 1)
+        d.dma_start(T.y[:, y0:y0 + w], T.ob[:, y0:y0 + w]).then_inc(sem["st%d" % b], 16)
+    for n, b in enumerate(done):
+        dq[n % 2].wait_ge(sem["st%d" % b], 16)

@@ -4,7 +4,6 @@ from concourse.mybir import dt
 N, GR, GC, KT, NC, CH = 10, 5, 2, 4, 128, 320
 XH0, XH1, XO, WO, WP, XF = 0, 256, 512, 1024, 1536, 2048
 QCOLS = XF + 4 * 512
-NO, NE = 0, 0
 
 SCRATCH = {
     "xb": ("sbuf", [128, 2048], "bfloat16"),
@@ -14,8 +13,8 @@ SCRATCH = {
     "ob": ("sbuf", [128, CH], "float32"),
     "ps": ("psum", [128, 3 * 512], "float32"),
 }
-SEMAPHORES = (["lx0", "lx1", "lw0", "lw1", "qx0", "qx1", "qw0", "qw1", "aw", "sent", "rl", "f0", "f1"]
-              + ["%s%d" % (n, j) for n in "aeo" for j in range(6)]
+SEMAPHORES = (["lx0", "lx1", "lw0", "lw1", "qx0", "qx1", "qw0", "qw1", "aw", "sent"]
+              + ["%s%d" % (n, j) for n in "ab" for j in range(6)]
               + ["%s%d" % (n, b) for n in ("mm", "cp", "st") for b in range(3)])
 MEMO = {}
 
@@ -45,10 +44,10 @@ def slot(i, c, g, kk):
     full = [b[0] for b in blocks(c) if b[2] == NC]
     if g in full:
         j = 2 * full.index(g) + kk
-        return XF + 512 * j, "a%d" % (2 + j)
+        return XF + 512 * j, 2 + j
     if i == g or kk == 1:
-        return XH1, "a1"
-    return XH0, "a0"
+        return XH1, 1
+    return XH0, 0
 
 
 def row_at(g, k, r):
@@ -59,131 +58,65 @@ def bits(m):
     return [b for b in range(m.bit_length()) if (m >> b) & 1]
 
 
-def lane_of(t):
-    return "o" if t < NO else "e" if t < NO + NE else "a"
-
-
 def plan_all(cores, topo):
-    calls = {}
-    every = range(topo.CHIPS * topo.CORES_PER_CHIP)
-
-    def add(core, order, waits, pool, trs):
-        calls.setdefault(core, []).append((order, waits, pool, trs))
-
-    def on(ch):
-        return [c for c in every if topo.chip(c) == ch]
-
-    def mate_of(ch):
-        return [m for m in range(topo.CHIPS) if topo.mates(ch, m)][0]
-
-    lanes = {"o": (0, NO), "e": (NO, NE), "a": (NO + NE, KT - NO - NE)}
+    calls, lands, need = {}, {}, {}
     for s in range(N):
         g, k = divmod(s, GC)
         me, mate = cores[s], cores[g * GC + (1 - k)]
         lo = bits(topo.mask(me, cores[row_at(g, k, 1) * GC + k]))
         hi = [b for b in bits(topo.mask(me, mate)) if b not in lo]
         S = seg_src(g, k)
-        free = [c for c in on(topo.chip(me)) if topo.die(c) == topo.die(me) and c not in cores]
-        port = [c for c in free if topo.may_write(c, on(mate_of(topo.chip(me)))[0])]
-        relay = {"o": port[0], "e": [c for c in free if c != port[0]][0]}
+        clock = [0]
 
-        def far(lane, r, base=None):
-            i, (t0, n), out = row_at(g, k, r), lanes[lane], []
+        def add(waits, pool, trs):
+            calls.setdefault(me, []).append((waits, pool, trs))
+            if pool is not hi:
+                clock[0] += sum(t[2] * (4 if t[0] == "q" else 1) for t in trs)
+            for (buf, sc, nc, d, dc, sn) in trs:
+                lands.setdefault(d, []).append((buf, dc, dc + nc, sn, clock[0] + (600 if pool is hi else 0)))
+                need.setdefault(d, {})
+                need[d][sn] = need[d].get(sn, 0) + len(pool) // len(trs)
+
+        def far(buf, r, part=None):
+            i, out = row_at(g, k, r), []
             for (c, off, w, sc) in S:
-                dc, sn = slot(i, c, g, k)
-                out.append(("q", sc + w * t0 if base is None else base, w * n, cores[i * GC + c], (dc + w * t0, lane + sn[1:])))
-                if base is not None:
-                    base += w * n
+                dc, j = slot(i, c, g, k)
+                for h in range(2):
+                    a, b = max(sc, XO + 256 * h), min(sc + KT * w, XO + 256 * h + 256)
+                    if b > a and part in (None, h):
+                        if part is None and out and out[-1][3] == cores[i * GC + c]:
+                            out[-1] = out[-1][:2] + (out[-1][2] + b - a,) + out[-1][3:]
+                        else:
+                            out.append((buf, a, b - a, cores[i * GC + c], dc + a - sc, "%s%d" % ("b" if part == 1 else "a", j)))
             return out
 
-        def planes(r):
-            i = row_at(g, k, r)
-            return [("p", sc, KT * w, cores[i * GC + c], slot(i, c, g, k)) for (c, off, w, sc) in S]
-
-        for lane in ("o", "e"):
-            t0, n = lanes[lane]
-            if n:
-                trs, rc = [], 0
-                for (c, off, w, sc) in S:
-                    trs.append(("q", sc + w * t0, w * n, relay[lane], (rc, "rl")))
-                    rc += w * n
-                add(me, 0, ["x"], hi, trs)
-                for r in range(1, GR):
-                    R, dest = relay[lane], cores[row_at(g, k, r) * GC + k]
-                    if lane == "e":
-                        add(R, r, ["rl"], bits(topo.mask(R, dest)), far("e", r, 0))
-                    else:
-                        F = [c for c in on(mate_of(topo.chip(dest))) if topo.die(c) == topo.die(R) and topo.may_write(c, dest)]
-                        f, j = F[(r - 1) % len(F)], (r - 1) // len(F)
-                        add(R, r, ["rl"], bits(topo.mask(R, f)), [("q", 0, rc, f, (rc * j, "f%d" % j))])
-                        add(f, r, ["f%d" % j], bits(topo.mask(f, dest)), far("o", r, rc * j))
-        add(me, 1, ["x"], lo, far("a", 1))
-        add(me, 2, ["x"], lo, [t for r in range(1, GR) for t in planes(r)])
-        add(me, 3, ["x"], lo, far("a", 2))
+        add(["qx0"], lo[:len(lo) // 2], far("q", 1, 0))
+        add(["qx1"], lo[len(lo) // 2:], far("q", 1, 1))
+        add([], lo, [t for r in range(1, GR) for t in far("p", r)])
+        add([], lo, far("q", 2))
         for buf in ("q", "p"):
-            tx = [(buf, sc, KT * w, mate, slot(g, c, g, k)) for (c, off, w, sc) in S if c != k]
-            tw = [(buf, WO, 512, mate, (WP, "aw"))]
+            tx = [(buf, sc, KT * w, mate) + (slot(g, c, g, k)[0], "a%d" % slot(g, c, g, k)[1]) for (c, off, w, sc) in S if c != k]
+            tw = [(buf, WO, 512, mate, WP, "aw")]
             if tx and tx[0][2] == 512:
-                add(me, 4, ["w"], hi, tx + tw)
+                add(["qw0", "qw1"], hi, tx + tw)
             else:
                 if tx:
-                    add(me, 4, ["x"], hi, tx)
-                add(me, 4, ["w"], hi, tw)
-        add(me, 5, ["x"], lo, far("a", 3))
-        add(me, 6, ["x"], lo, far("a", 4))
-    need = {}
-    for c in calls:
-        calls[c].sort(key=lambda x: x[0])
-        for (_, _, pool, trs) in calls[c]:
-            for t in trs:
-                d = need.setdefault(t[3], {})
-                d[t[4][1]] = d.get(t[4][1], 0) + len(pool) // len(trs)
-    return calls, need
-
-
-def send_all(g, T, topo, calls, need):
-    sem = T.sem
-    waited, sent = set(), 0
-    for (_, waits, pool, trs) in calls:
-        for key in waits:
-            if key not in waited:
-                waited.add(key)
-                if key in ("x", "w"):
-                    for h in range(2):
-                        g.wait_ge(sem["q%s%d" % (key, h)], 1)
-                else:
-                    g.wait_ge(sem[key], need[key])
-        n = len(pool) // len(trs)
-        out = []
-        for j, (buf, sc, nc, d, (dc, sn)) in enumerate(trs):
-            mask = sum(1 << b for b in pool[j * n:(j + 1) * n])
-            if buf == "q":
-                src, dst = T.q[:, sc:sc + nc].bitcast(dt.uint8), T.q[:, dc:dc + nc].bitcast(dt.uint8)
-            else:
-                src, dst = T.p[:, sc:sc + nc], T.p[:, dc:dc + nc]
-            rid, pid, _ = topo.addr(d)
-            out.append((src, dst, rid, pid, mask, sem[sn]))
-            sent += n
-        if len(out) == 1:
-            src, dst, rid, pid, mask, sn = out[0]
-            g.remote_dma(out_ap=dst, in_ap=src, remote_sem=sn, local_sem=sem.sent, pid=pid, routing_id=rid, dma_engine_mask=mask)
-        else:
-            g.remote_dma_fused([RemoteDMATransfer(dst_ids=[DstId(rid=rid, pnc=pid)], dma_engine_mask=mask, remote_sem=sn, src=src, dst=dst)
-                                for (src, dst, rid, pid, mask, sn) in out], local_sem=sem.sent)
-    g.wait_ge(sem.sent, sent)
+                    add([], hi, tx)
+                add(["qw0", "qw1"], hi, tw)
+        add([], lo, far("q", 3))
+        add([], lo, far("q", 4, 0))
+        add([], lo, far("q", 4, 1))
+    return calls, lands, need
 
 
 def rank_program(g, core, T, topo):
+    r = T.rank_of(core)
+    if r is None:
+        return
     cores = list(T.cores)
     if "plan" not in MEMO:
         MEMO["plan"] = plan_all(cores, topo)
-    calls, needs = MEMO["plan"]
-    need = needs.get(core, {})
-    r = T.rank_of(core)
-    if r is None:
-        if core in calls:
-            send_all(g, T, topo, calls[core], need)
-        return
+    calls, lands, need = (d[core] for d in MEMO["plan"])
     i, k = divmod(r, GC)
     sem = T.sem
 
@@ -209,43 +142,51 @@ def rank_program(g, core, T, topo):
             a = col + 256 * h
             v.quantize_mx(T.q[:, a:a + 256], T.p[:, a:a + 256], buf[:, 1024 * h:1024 * h + 1024]).then_inc(sem["q%s%d" % (nm, h)], 1)
 
-    send_all(g, T, topo, calls[core], need)
-
-    def due(lane, gg, kk):
-        st = [row_at(gg, kk, q) for q in range(GR)].index(i)
-        return {"a": 1 + st * (KT - NO - NE), "e": 5 + st * NE, "o": 9 + (st + 1) * NO}[lane]
+    sent = 0
+    for (waits, pool, trs) in calls:
+        for nm in waits:
+            g.wait_ge(sem[nm], 1)
+        n = len(pool) // len(trs)
+        out = []
+        for j, (buf, sc, nc, d, dc, sn) in enumerate(trs):
+            mask = sum(1 << b for b in pool[j * n:(j + 1) * n])
+            if buf == "q":
+                src, dst = T.q[:, sc:sc + nc].bitcast(dt.uint8), T.q[:, dc:dc + nc].bitcast(dt.uint8)
+            else:
+                src, dst = T.p[:, sc:sc + nc], T.p[:, dc:dc + nc]
+            rid, pid, _ = topo.addr(d)
+            out.append((src, dst, rid, pid, mask, sem[sn]))
+            sent += n
+        if len(out) == 1:
+            src, dst, rid, pid, mask, sn = out[0]
+            g.remote_dma(out_ap=dst, in_ap=src, remote_sem=sn, local_sem=sem.sent, pid=pid, routing_id=rid, dma_engine_mask=mask)
+        else:
+            g.remote_dma_fused([RemoteDMATransfer(dst_ids=[DstId(rid=rid, pnc=pid)], dma_engine_mask=mask, remote_sem=sn, src=src, dst=dst)
+                                for (src, dst, rid, pid, mask, sn) in out], local_sem=sem.sent)
+    g.wait_ge(sem.sent, sent)
 
     ops = []
     for b, (gg, off, w) in enumerate(blocks(k)):
         for kk in range(GC):
-            col, sn = slot(i, k, gg, kk)
+            col = slot(i, k, gg, kk)[0]
             for t in range(KT):
-                deps, est = [sn], 0 if sn is None else 1
-                if gg != i:
-                    deps.append(lane_of(t) + sn[1:])
-                    est = max(due("a", gg, kk), due(lane_of(t), gg, kk))
-                if kk != k:
-                    deps.append("aw")
-                    est = max(est, 1)
-                if w < NC and t == KT - 1 and col == XH0:
-                    deps += ["a1", lane_of(0) + "1"]
-                    est = max(est, due("a", gg, 1), due(lane_of(0), gg, 1))
-                ops.append((est, b, kk, t, col + w * t, deps))
+                wc, xc = (WO if kk == k else WP) + NC * t, col + w * t
+                hit = [l for l in lands if any(l[1] < a + NC and a < l[2] for a in (wc, xc))]
+                ops.append((max([l[4] for l in hit] + [0]), b, kk, t, wc, xc, sorted(set(l[3] for l in hit))))
     ops.sort(key=lambda o: o[:4])
     te = g.tensor
     for nm in ("qx0", "qx1", "qw0", "qw1"):
         te.wait_ge(sem[nm], 1)
     seen, done = set(), []
-    for n, (est, b, kk, t, col, deps) in enumerate(ops):
+    for n, (est, b, kk, t, wc, xc, deps) in enumerate(ops):
         for sn in deps:
-            if sn is not None and sn not in seen:
+            if sn not in seen:
                 seen.add(sn)
                 te.wait_ge(sem[sn], need[sn])
         first = not any(o[1] == b for o in ops[:n])
         last = not any(o[1] == b for o in ops[n + 1:])
-        wc = (WO if kk == k else WP) + NC * t
         ins = te.matmul_mx(T.ps[:, 512 * b:512 * b + NC], T.q[:, wc:wc + NC], T.p[:, wc:wc + NC],
-                           T.q[:, col:col + NC], T.p[:, col:col + NC], first, last)
+                           T.q[:, xc:xc + NC], T.p[:, xc:xc + NC], first, last)
         if last:
             ins.then_inc(sem["mm%d" % b], 1)
             done.append(b)

@@ -1,9 +1,11 @@
 from concourse.bass import DstId, RemoteDMATransfer
-from concourse.mybir import dt
+from concourse.mybir import dt, AluOpType
 
 N, GR, GC, KT, NC, CH = 10, 5, 2, 4, 128, 320
-XH0, XH1, XO, WO, WP, XF = 0, 256, 512, 1024, 1536, 2048
-QCOLS = XF + 4 * 512
+DW, DX1, DX2 = 1, 3, 1
+XO, XD, WO, WP, WA, XR, XL = 1024, 1536, 2048, 2560, 3072, 3584, 4096
+QCOLS = XL + 2 * 512
+NB = 7
 
 SCRATCH = {
     "xb": ("sbuf", [128, 2048], "bfloat16"),
@@ -11,11 +13,15 @@ SCRATCH = {
     "q": ("sbuf", [128, QCOLS], "float8_e4m3fn_x4"),
     "p": ("sbuf", [128, QCOLS], "uint8"),
     "ob": ("sbuf", [128, CH], "float32"),
-    "ps": ("psum", [128, 3 * 512], "float32"),
+    "sb": ("sbuf", [128, NB * NC], "float32"),
+    "l0": ("sbuf", [128, CH], "float32"),
+    "l1": ("sbuf", [128, CH], "float32"),
+    "ps": ("psum", [128, NB * 512], "float32"),
 }
-SEMAPHORES = (["lx0", "lx1", "lw0", "lw1", "qx0", "qx1", "qw0", "qw1", "aw", "sent"]
-              + ["%s%d" % (n, j) for n in "ab" for j in range(6)]
-              + ["%s%d" % (n, b) for n in ("mm", "cp", "st") for b in range(3)])
+SEMAPHORES = (["lx0", "lx1", "lw0", "lw1", "qx0", "qx1", "qw0", "qw1", "aw", "da", "db", "xa", "xb", "xr",
+               "la0", "la1", "lb0", "lb1", "sent"]
+              + ["%s%d" % (n, b) for n in ("mm", "cp") for b in range(NB)]
+              + ["%s%d" % (n, b) for n in ("st", "f", "ad") for b in range(3)])
 MEMO = {}
 
 
@@ -38,20 +44,49 @@ def seg_src(g, k):
     return out
 
 
-def slot(i, c, g, kk):
-    if (i, c) == (g, kk):
-        return XO, None
-    full = [b[0] for b in blocks(c) if b[2] == NC]
-    if g in full:
-        j = 2 * full.index(g) + kk
-        return XF + 512 * j, 2 + j
-    if i == g or kk == 1:
-        return XH1, 1
-    return XH0, 0
+def xcol(c, k, g, kk, cc):
+    S = seg_src(g, kk)
+    whole = len(S) == 1
+    sc = [s[3] for s in S if s[0] == cc][0]
+    if g == c:
+        return sc
+    if g == (c + DX1) % GR:
+        if kk == k:
+            return (XD if whole else XO - 512) + sc - XO
+        return XR if whole else XO - 768
+    return XL + 512 * kk if whole else XO - 512 + 256 * kk
 
 
-def row_at(g, k, r):
-    return (g + r) % GR if k == 0 else (g - r) % GR
+def jobs_all():
+    J = {(c, k): [] for c in range(GR) for k in range(GC)}
+    for i in range(GR):
+        for cc in range(GC):
+            for (g, off, w) in blocks(cc):
+                d = (g - i) % GR
+                if d in (DX1, DX2):
+                    J[(i, cc)].append((i, g, off, w, cc, tuple(range(GC))))
+                else:
+                    for k in range(GC):
+                        J[(i if d == 0 else (i - DW) % GR, k)].append((i, g, off, w, cc, (k,)))
+    return J
+
+
+def ops_for(c, k, J, L):
+    ops = []
+    for b, (i, gg, off, w, cc, kks) in enumerate(J):
+        for kk in kks:
+            col = xcol(c, k, gg, kk, cc)
+            for t in range(KT):
+                wc = ((WO if kk == k else WP) if i == c else WA) + NC * t
+                xc = col + w * t
+                hit = [l for l in L if l[0] in ("q", "p") and any(l[1] < a + NC and a < l[2] for a in (wc, xc))]
+                ops.append((max([l[4] for l in hit] + [0]), int(i == c), b, kk, t, wc, xc, sorted(set(l[3] for l in hit))))
+    ops.sort(key=lambda o: o[:5])
+    return ops
+
+
+def finish_order(ops):
+    return [o[2] for n, o in enumerate(ops) if not any(p[2] == o[2] for p in ops[n + 1:])]
 
 
 def bits(m):
@@ -59,54 +94,70 @@ def bits(m):
 
 
 def plan_all(cores, topo):
-    calls, lands, need = {}, {}, {}
+    calls, lands, need, J = {}, {}, {}, jobs_all()
+
+    def add(me, waits, pool, trs, est):
+        for wd in sorted(set(t[2] for t in trs), reverse=True):
+            grp = [t for t in trs if t[2] == wd]
+            calls.setdefault(me, []).append((waits, pool, grp))
+            waits = []
+            for (buf, sc, nc, d, dc, sn) in grp:
+                lands.setdefault(d, []).append((buf, dc, dc + nc, sn, est))
+                need.setdefault(d, {})
+                need[d][sn] = need[d].get(sn, 0) + len(pool) // len(grp)
+
+    def floats(c, k, sel):
+        w8, trs = [], []
+        for b, (i, gg, off, w, cc, kks) in enumerate(J[(c, k)]):
+            if (i, cc) != (c, k) and sel(i):
+                w8.append("cp%d" % b)
+                trs.append((("sb", "l%d" % k), NC * b, w, cores[i * GC + cc], NC * gg + off - CH * cc, "f%d" % blocks(cc).index((gg, off, w))))
+        return w8, trs
+
     for s in range(N):
         g, k = divmod(s, GC)
         me, mate = cores[s], cores[g * GC + (1 - k)]
-        lo = bits(topo.mask(me, cores[row_at(g, k, 1) * GC + k]))
+        up, mid = (g - DW) % GR, (g - DX1) % GR
+        lo = bits(topo.mask(me, cores[up * GC + k]))
         hi = [b for b in bits(topo.mask(me, mate)) if b not in lo]
         S = seg_src(g, k)
-        clock = [0]
 
-        def add(waits, pool, trs):
-            calls.setdefault(me, []).append((waits, pool, trs))
-            if pool is not hi:
-                clock[0] += sum(t[2] * (4 if t[0] == "q" else 1) for t in trs)
-            for (buf, sc, nc, d, dc, sn) in trs:
-                lands.setdefault(d, []).append((buf, dc, dc + nc, sn, clock[0] + (600 if pool is hi else 0)))
-                need.setdefault(d, {})
-                need[d][sn] = need[d].get(sn, 0) + len(pool) // len(trs)
-
-        def far(buf, r, part=None):
-            i, out = row_at(g, k, r), []
+        def last(buf, part=None):
+            out = []
             for (c, off, w, sc) in S:
-                dc, j = slot(i, c, g, k)
+                dc = xcol(up, c, g, k, c)
                 for h in range(2):
                     a, b = max(sc, XO + 256 * h), min(sc + KT * w, XO + 256 * h + 256)
                     if b > a and part in (None, h):
-                        if part is None and out and out[-1][3] == cores[i * GC + c]:
+                        if part is None and out and out[-1][3] == cores[up * GC + c]:
                             out[-1] = out[-1][:2] + (out[-1][2] + b - a,) + out[-1][3:]
                         else:
-                            out.append((buf, a, b - a, cores[i * GC + c], dc + a - sc, "%s%d" % ("b" if part == 1 else "a", j)))
+                            out.append((buf, a, b - a, cores[up * GC + c], dc + a - sc, "l%s%d" % ("b" if part == 1 else "a", k)))
             return out
 
-        add(["qx0"], lo[:len(lo) // 2], far("q", 1, 0))
-        add(["qx1"], lo[len(lo) // 2:], far("q", 1, 1))
-        add([], lo, [t for r in range(1, GR) for t in far("p", r)])
-        add([], lo, far("q", 2))
-        for buf in ("q", "p"):
-            tx = [(buf, sc, KT * w, mate) + (slot(g, c, g, k)[0], "a%d" % slot(g, c, g, k)[1]) for (c, off, w, sc) in S if c != k]
-            tw = [(buf, WO, 512, mate, WP, "aw")]
-            if tx and tx[0][2] == 512:
-                add(["qw0", "qw1"], hi, tx + tw)
-            else:
-                if tx:
-                    add([], hi, tx)
-                add(["qw0", "qw1"], hi, tw)
-        add([], lo, far("q", 3))
-        add([], lo, far("q", 4, 0))
-        add([], lo, far("q", 4, 1))
-    return calls, lands, need
+        md, mc = cores[mid * GC + k], xcol(mid, k, g, k, S[0][0])
+        ud = cores[up * GC + k]
+        add(me, ["qx0"], lo[:len(lo) // 2], [("q", XO, 256, md, mc, "xa")], 2)
+        add(me, ["qx1"], lo[len(lo) // 2:], [("q", XO + 256, 256, md, mc + 256, "xb")], 3)
+        add(me, [], lo, [("p", XO, 512, md, mc, "xa")], 2)
+        for n, buf in enumerate(("q", "p")):
+            add(me, [] if n else ["qw0", "qw1"], hi, [(buf, WO, 512, mate, WP, "aw")], 1)
+        add(me, [], lo, [("p", WO, 512, ud, WA, "da")] + last("p"), 4)
+        add(me, [], lo, [("q", WO, 256, ud, WA, "da")], 4)
+        add(me, [], lo, [("q", WO + 256, 256, ud, WA + 256, "db")], 6)
+        w8, trs = floats(g, k, lambda i: i == g)
+        if trs:
+            add(me, w8, hi, trs, 0)
+        b1 = (g + DX1) % GR
+        for n, buf in enumerate(("q", "p")):
+            tx = [(buf, xcol(g, k, b1, k, c), KT * w, mate, xcol(g, c, b1, k, c), "xr") for (c, off, w, sc) in seg_src(b1, k) if c != k]
+            if tx:
+                add(me, [] if n else ["xa", "xb"], hi, tx, 7)
+        add(me, [], lo, last("q", 0), 8)
+        add(me, [], lo, last("q", 1), 9)
+        w8, trs = floats(g, k, lambda i: i != g)
+        add(me, w8, lo, trs, 0)
+    return calls, lands, need, J
 
 
 def rank_program(g, core, T, topo):
@@ -116,8 +167,9 @@ def rank_program(g, core, T, topo):
     cores = list(T.cores)
     if "plan" not in MEMO:
         MEMO["plan"] = plan_all(cores, topo)
-    calls, lands, need = (d[core] for d in MEMO["plan"])
+    calls, lands, need = (d[core] for d in MEMO["plan"][:3])
     i, k = divmod(r, GC)
+    J = MEMO["plan"][3][(i, k)]
     sem = T.sem
 
     dq = [g.sync, g.scalar]
@@ -145,15 +197,17 @@ def rank_program(g, core, T, topo):
     sent = 0
     for (waits, pool, trs) in calls:
         for nm in waits:
-            g.wait_ge(sem[nm], 1)
+            g.wait_ge(sem[nm], need.get(nm, 1))
         n = len(pool) // len(trs)
         out = []
         for j, (buf, sc, nc, d, dc, sn) in enumerate(trs):
             mask = sum(1 << b for b in pool[j * n:(j + 1) * n])
             if buf == "q":
                 src, dst = T.q[:, sc:sc + nc].bitcast(dt.uint8), T.q[:, dc:dc + nc].bitcast(dt.uint8)
-            else:
+            elif buf == "p":
                 src, dst = T.p[:, sc:sc + nc], T.p[:, dc:dc + nc]
+            else:
+                src, dst = T[buf[0]][:, sc:sc + nc], T[buf[1]][:, dc:dc + nc]
             rid, pid, _ = topo.addr(d)
             out.append((src, dst, rid, pid, mask, sem[sn]))
             sent += n
@@ -165,39 +219,60 @@ def rank_program(g, core, T, topo):
                                 for (src, dst, rid, pid, mask, sn) in out], local_sem=sem.sent)
     g.wait_ge(sem.sent, sent)
 
-    ops = []
-    for b, (gg, off, w) in enumerate(blocks(k)):
-        for kk in range(GC):
-            col = slot(i, k, gg, kk)[0]
-            for t in range(KT):
-                wc, xc = (WO if kk == k else WP) + NC * t, col + w * t
-                hit = [l for l in lands if any(l[1] < a + NC and a < l[2] for a in (wc, xc))]
-                ops.append((max([l[4] for l in hit] + [0]), b, kk, t, wc, xc, sorted(set(l[3] for l in hit))))
-    ops.sort(key=lambda o: o[:4])
+    ops = ops_for(i, k, J, lands)
+    done = finish_order(ops)
     te = g.tensor
     for nm in ("qx0", "qx1", "qw0", "qw1"):
         te.wait_ge(sem[nm], 1)
-    seen, done = set(), []
-    for n, (est, b, kk, t, wc, xc, deps) in enumerate(ops):
+    seen = set()
+    for n, (est, own, b, kk, t, wc, xc, deps) in enumerate(ops):
         for sn in deps:
             if sn not in seen:
                 seen.add(sn)
                 te.wait_ge(sem[sn], need[sn])
-        first = not any(o[1] == b for o in ops[:n])
-        last = not any(o[1] == b for o in ops[n + 1:])
+        first = not any(o[2] == b for o in ops[:n])
+        last = not any(o[2] == b for o in ops[n + 1:])
         ins = te.matmul_mx(T.ps[:, 512 * b:512 * b + NC], T.q[:, wc:wc + NC], T.p[:, wc:wc + NC],
                            T.q[:, xc:xc + NC], T.p[:, xc:xc + NC], first, last)
         if last:
             ins.then_inc(sem["mm%d" % b], 1)
-            done.append(b)
 
-    for n, b in enumerate(done):
-        gg, off, w = blocks(k)[b]
-        y0 = NC * gg + off - CH * k
+    mine = blocks(k)
+    stays = [b for b in done if (J[b][0], J[b][4]) == (i, k) and len(J[b][5]) < GC]
+    seq = [b for b in done if b not in stays]
+    at = [n for n, b in enumerate(seq) if (J[b][1] - i) % GR == DX2 and J[b][0] == i]
+    at = at[0] if at else len(seq)
+    ready = {}
+    for b in seq[:at] + stays + seq[at:]:
+        ii, gg, off, w, cc, kks = J[b]
         v.wait_ge(sem["mm%d" % b], 1)
-        v.tensor_copy(T.ob[:, y0:y0 + w], T.ps[:, 512 * b:512 * b + w]).then_inc(sem["cp%d" % b], 1)
+        acc = T.ps[:, 512 * b:512 * b + w]
+        if (ii, cc) != (i, k):
+            ins = v.tensor_copy(T.sb[:, NC * b:NC * b + w], acc)
+        else:
+            y0 = NC * gg + off - CH * k
+            ready[(gg, off, w)] = "cp%d" % b
+            if b in stays:
+                fs = "f%d" % mine.index((gg, off, w))
+                v.wait_ge(sem[fs], need[fs])
+                ins = v.tensor_tensor(T.ob[:, y0:y0 + w], acc, T["l%d" % (1 - k)][:, y0:y0 + w], AluOpType.add)
+            else:
+                ins = v.tensor_copy(T.ob[:, y0:y0 + w], acc)
+        ins.then_inc(sem["cp%d" % b], 1)
+    for bi, (gg, off, w) in enumerate(mine):
+        if (gg, off, w) not in ready:
+            y0 = NC * gg + off - CH * k
+            v.wait_ge(sem["f%d" % bi], need["f%d" % bi])
+            v.tensor_tensor(T.ob[:, y0:y0 + w], T.l0[:, y0:y0 + w], T.l1[:, y0:y0 + w], AluOpType.add).then_inc(sem["ad%d" % bi], 1)
+            ready[(gg, off, w)] = "ad%d" % bi
+
+    when = {DX1: 0, 0: 1, DX2: 2}
+    todo = sorted(enumerate(mine), key=lambda e: when.get((e[1][0] - i) % GR, 3))
+    for n, (bi, blk) in enumerate(todo):
+        gg, off, w = blk
+        y0 = NC * gg + off - CH * k
         d = dq[n % 2]
-        d.wait_ge(sem["cp%d" % b], 1)
-        d.dma_start(T.y[:, y0:y0 + w], T.ob[:, y0:y0 + w]).then_inc(sem["st%d" % b], 16)
-    for n, b in enumerate(done):
-        dq[n % 2].wait_ge(sem["st%d" % b], 16)
+        d.wait_ge(sem[ready[blk]], 1)
+        d.dma_start(T.y[:, y0:y0 + w], T.ob[:, y0:y0 + w]).then_inc(sem["st%d" % bi], 16)
+    for n, (bi, blk) in enumerate(todo):
+        dq[n % 2].wait_ge(sem["st%d" % bi], 16)

@@ -6,6 +6,7 @@ DW, DX1, DX2 = 1, 3, 1
 XO, XD, WO, WP, WA, XR, XL = 1024, 1536, 2048, 2560, 3072, 3584, 4096
 QCOLS = XL + 2 * 512
 NB = 7
+NSIM = 80
 
 SCRATCH = {
     "xb": ("sbuf", [128, 2048], "bfloat16"),
@@ -18,8 +19,8 @@ SCRATCH = {
     "l1": ("sbuf", [128, CH], "float32"),
     "ps": ("psum", [128, NB * 512], "float32"),
 }
-SEMAPHORES = (["lx0", "lx1", "lw0", "lw1", "qx0", "qx1", "qw0", "qw1", "aw", "da", "db", "xa", "xb", "xr",
-               "la0", "la1", "lb0", "lb1", "sent"]
+SEMAPHORES = (["aw", "xa", "xb", "xr", "la0", "la1", "lb0", "lb1", "sent", "h0", "h1", "hp0", "dp0", "dp1"]
+              + ["%s%d" % (n, b) for n in ("lx", "qx", "lw", "qw", "d") for b in range(4)]
               + ["%s%d" % (n, b) for n in ("mm", "cp") for b in range(NB)]
               + ["%s%d" % (n, b) for n in ("st", "f", "ad") for b in range(3)])
 MEMO = {}
@@ -93,6 +94,10 @@ def bits(m):
     return [b for b in range(m.bit_length()) if (m >> b) & 1]
 
 
+def lane(pool, n):
+    return pool if n is None else pool[n * len(pool) // 2:(n + 1) * len(pool) // 2]
+
+
 def plan_all(cores, topo):
     calls, lands, need, J = {}, {}, {}, jobs_all()
 
@@ -121,30 +126,43 @@ def plan_all(cores, topo):
         lo = bits(topo.mask(me, cores[up * GC + k]))
         hi = [b for b in bits(topo.mask(me, mate)) if b not in lo]
         S = seg_src(g, k)
-
-        def last(buf, part=None):
-            out = []
-            for (c, off, w, sc) in S:
-                dc = xcol(up, c, g, k, c)
-                for h in range(2):
-                    a, b = max(sc, XO + 256 * h), min(sc + KT * w, XO + 256 * h + 256)
-                    if b > a and part in (None, h):
-                        if part is None and out and out[-1][3] == cores[up * GC + c]:
-                            out[-1] = out[-1][:2] + (out[-1][2] + b - a,) + out[-1][3:]
-                        else:
-                            out.append((buf, a, b - a, cores[up * GC + c], dc + a - sc, "l%s%d" % ("b" if part == 1 else "a", k)))
-            return out
-
         md, mc = cores[mid * GC + k], xcol(mid, k, g, k, S[0][0])
         ud = cores[up * GC + k]
-        add(me, ["qx0"], lo[:len(lo) // 2], [("q", XO, 256, md, mc, "xa")], 2)
-        add(me, ["qx1"], lo[len(lo) // 2:], [("q", XO + 256, 256, md, mc + 256, "xb")], 3)
+        rc = [c for c in range(NSIM) if topo.mates(topo.chip(c), topo.chip(ud)) and topo.die(c) == topo.die(me)
+              and topo.may_write(c, ud)][0]
+        hc = [c for c in range(NSIM) if topo.chip(c) == topo.chip(me) and topo.die(c) == topo.die(me) and c not in cores
+              and topo.may_write(c, rc)][0]
+
+        def owner(a):
+            (c, off, ws, sc) = [e for e in S if e[3] <= a < e[3] + KT * e[2]][0]
+            return cores[up * GC + c], xcol(up, c, g, k, c) + a - sc
+
+        def hand(buf, a, w, sn, ln):
+            own, dc = owner(a)
+            add(me, [], lane(hi, ln), [(buf, a, w, hc, a, sn)], 0)
+            add(hc, [sn], lane(bits(topo.mask(hc, rc)), ln), [(buf, a, w, rc, a, sn)], 0)
+            add(rc, [sn], lane(bits(topo.mask(rc, own)), ln), [(buf, a, w, own, dc, "la%d" % k)], 8)
+
+        for j in range(4):
+            add(me, ["qx%d" % j], lane(lo, j % 2), [("q", XO + 128 * j, 128, md, mc + 128 * j, "xa" if j < 2 else "xb")], 2 + j // 2)
+            if j < 2:
+                hand("q", XO + 128 * j, 128, "h%d" % j, j)
+            if j == 1:
+                hand("p", XO, 256, "hp0", None)
         add(me, [], lo, [("p", XO, 512, md, mc, "xa")], 2)
-        for n, buf in enumerate(("q", "p")):
-            add(me, [] if n else ["qw0", "qw1"], hi, [(buf, WO, 512, mate, WP, "aw")], 1)
-        add(me, [], lo, [("p", WO, 512, ud, WA, "da")] + last("p"), 4)
-        add(me, [], lo, [("q", WO, 256, ud, WA, "da")], 4)
-        add(me, [], lo, [("q", WO + 256, 256, ud, WA + 256, "db")], 6)
+
+        def both(buf, a, w, sn, waits, est):
+            add(me, waits, lo + hi, [(buf, WO + a, w, ud, WA + a, sn), (buf, WO + a, w, mate, WP + a, "aw")], est)
+
+        for j in range(4):
+            w8 = ["qw%d" % j]
+            if j % 2:
+                both("p", 128 * (j - 1), 256, "dp%d" % (j // 2), w8, 3.75 + 0.5 * j)
+                w8 = []
+            both("q", 128 * j, 128, "d%d" % j, w8, 4 + 0.5 * j)
+        own, dc = owner(XO + 256)
+        for buf in ("p", "q"):
+            add(me, [], lo, [(buf, XO + 256, 256, own, dc, "lb%d" % k)], 9)
         w8, trs = floats(g, k, lambda i: i == g)
         if trs:
             add(me, w8, hi, trs, 0)
@@ -153,47 +171,13 @@ def plan_all(cores, topo):
             tx = [(buf, xcol(g, k, b1, k, c), KT * w, mate, xcol(g, c, b1, k, c), "xr") for (c, off, w, sc) in seg_src(b1, k) if c != k]
             if tx:
                 add(me, [] if n else ["xa", "xb"], hi, tx, 7)
-        add(me, [], lo, last("q", 0), 8)
-        add(me, [], lo, last("q", 1), 9)
         w8, trs = floats(g, k, lambda i: i != g)
         add(me, w8, lo, trs, 0)
     return calls, lands, need, J
 
 
-def rank_program(g, core, T, topo):
-    r = T.rank_of(core)
-    if r is None:
-        return
-    cores = list(T.cores)
-    if "plan" not in MEMO:
-        MEMO["plan"] = plan_all(cores, topo)
-    calls, lands, need = (d[core] for d in MEMO["plan"][:3])
-    i, k = divmod(r, GC)
-    J = MEMO["plan"][3][(i, k)]
+def remote_calls(g, T, topo, calls, need):
     sem = T.sem
-
-    dq = [g.sync, g.scalar]
-    S = seg_src(i, k)
-    if len(S) == 1:
-        for h in range(2):
-            dq[h].dma_start(T.xb[:, 1024 * h:1024 * h + 1024], T.x[:, 1024 * h:1024 * h + 1024]).then_inc(sem["lx%d" % h], 16)
-        nl = 16
-    else:
-        for j, (c, off, w, sc) in enumerate(S):
-            for t in range(KT):
-                a = 4 * (sc - XO) + 4 * w * t
-                dq[t // 2].dma_start(T.xb[:, a:a + 4 * w], T.x[:, 512 * t + 4 * off:512 * t + 4 * off + 4 * w]).then_inc(sem["lx%d" % j], 16)
-        nl = 16 * KT
-    for h in range(2):
-        dq[h].dma_start(T.wb[:, 1024 * h:1024 * h + 1024], T.w[:, 1024 * h:1024 * h + 1024]).then_inc(sem["lw%d" % h], 16)
-
-    v = g.vector
-    for (nm, buf, col, cnt) in (("x", T.xb, XO, nl), ("w", T.wb, WO, 16)):
-        for h in range(2):
-            v.wait_ge(sem["l%s%d" % (nm, h)], cnt)
-            a = col + 256 * h
-            v.quantize_mx(T.q[:, a:a + 256], T.p[:, a:a + 256], buf[:, 1024 * h:1024 * h + 1024]).then_inc(sem["q%s%d" % (nm, h)], 1)
-
     sent = 0
     for (waits, pool, trs) in calls:
         for nm in waits:
@@ -219,17 +203,49 @@ def rank_program(g, core, T, topo):
                                 for (src, dst, rid, pid, mask, sn) in out], local_sem=sem.sent)
     g.wait_ge(sem.sent, sent)
 
-    ops = ops_for(i, k, J, lands)
+
+def rank_program(g, core, T, topo):
+    cores = list(T.cores)
+    if "plan" not in MEMO:
+        MEMO["plan"] = plan_all(cores, topo)
+    if core not in MEMO["plan"][0]:
+        return
+    calls, lands, need = (d[core] for d in MEMO["plan"][:3])
+    r = T.rank_of(core)
+    if r is None:
+        remote_calls(g, T, topo, calls, need)
+        return
+    i, k = divmod(r, GC)
+    J = MEMO["plan"][3][(i, k)]
+    sem = T.sem
+
+    dq = [g.sync, g.scalar]
+    S = seg_src(i, k)
+    for m in range(8):
+        a = 256 * m if len(S) == 1 else 512 * (m % KT) + 4 * S[m // KT][1]
+        dq[m % 2].dma_start(T.xb[:, 256 * m:256 * m + 256], T.x[:, a:a + 256]).then_inc(sem["lx%d" % (m // 2)], 16)
+    for m in range(8):
+        dq[m % 2].dma_start(T.wb[:, 256 * m:256 * m + 256], T.w[:, 256 * m:256 * m + 256]).then_inc(sem["lw%d" % (m // 2)], 16)
+
+    v = g.vector
+    for (nm, buf, col) in (("x", T.xb, XO), ("w", T.wb, WO)):
+        for h in range(4):
+            v.wait_ge(sem["l%s%d" % (nm, h)], 32)
+            a = col + 128 * h
+            v.quantize_mx(T.q[:, a:a + 128], T.p[:, a:a + 128], buf[:, 512 * h:512 * h + 512]).then_inc(sem["q%s%d" % (nm, h)], 1)
+
+    remote_calls(g, T, topo, calls, need)
+
+    made = [("q", c0 + 128 * j, c0 + 128 * j + 128, "q%s%d" % (nm, j), e0 + 0.2 * j) for (nm, c0, e0) in (("x", XO, 0), ("w", WO, 3)) for j in range(4)]
+    ops = ops_for(i, k, J, lands + made)
     done = finish_order(ops)
     te = g.tensor
-    for nm in ("qx0", "qx1", "qw0", "qw1"):
-        te.wait_ge(sem[nm], 1)
     seen = set()
     for n, (est, own, b, kk, t, wc, xc, deps) in enumerate(ops):
         for sn in deps:
             if sn not in seen:
                 seen.add(sn)
-                te.wait_ge(sem[sn], need[sn])
+                te.wait_ge(sem[sn], need.get(sn, 1))
         first = not any(o[2] == b for o in ops[:n])
         last = not any(o[2] == b for o in ops[n + 1:])
         ins = te.matmul_mx(T.ps[:, 512 * b:512 * b + NC], T.q[:, wc:wc + NC], T.p[:, wc:wc + NC],

from concourse.bass import DstId, RemoteDMATransfer
from concourse.mybir import dt, AluOpType

N, GR, GC, KT, NC, CH = 10, 5, 2, 4, 128, 320
DW, DX1, DX2 = 1, 3, 1
XO, XD, WO, WP, WA, XR, XL = 1024, 1536, 2048, 2560, 3072, 3584, 4096
QCOLS = XL + 2 * 512
NB = 7
NSIM = 80

SCRATCH = {
    "xb": ("sbuf", [128, 2048], "bfloat16"),
    "wb": ("sbuf", [128, 2048], "bfloat16"),
    "q": ("sbuf", [128, QCOLS], "float8_e4m3fn_x4"),
    "p": ("sbuf", [128, QCOLS], "uint8"),
    "ob": ("sbuf", [128, CH], "float32"),
    "sb": ("sbuf", [128, NB * NC], "float32"),
    "l0": ("sbuf", [128, CH], "float32"),
    "l1": ("sbuf", [128, CH], "float32"),
    "ps": ("psum", [128, NB * 512], "float32"),
}
SEMAPHORES = (["aw", "xa", "xb", "xr", "la0", "la1", "lb0", "lb1", "sent", "h0", "h1", "hp0", "dp0", "dp1"]
              + ["%s%d" % (n, b) for n in ("lx", "qx", "lw", "qw", "d") for b in range(4)]
              + ["%s%d" % (n, b) for n in ("mm", "cp") for b in range(NB)]
              + ["%s%d" % (n, b) for n in ("st", "f", "ad") for b in range(3)])
MEMO = {}


def blocks(c):
    out = []
    for g in range(GR):
        lo, hi = max(NC * g, CH * c), min(NC * g + NC, CH * c + CH)
        if hi > lo:
            out.append((g, lo - NC * g, hi - lo))
    return out


def seg_src(g, k):
    segs = [(c, off, w) for c in range(GC) for (gg, off, w) in blocks(c) if gg == g]
    segs.sort(key=lambda s: s[0] != k)
    out, col = [], XO
    for (c, off, w) in segs:
        out.append((c, off, w, col))
        col += KT * w
    return out


def xcol(c, k, g, kk, cc):
    S = seg_src(g, kk)
    whole = len(S) == 1
    sc = [s[3] for s in S if s[0] == cc][0]
    if g == c:
        return sc
    if g == (c + DX1) % GR:
        if kk == k:
            return (XD if whole else XO - 512) + sc - XO
        return XR if whole else XO - 768
    return XL + 512 * kk if whole else XO - 512 + 256 * kk


def jobs_all():
    J = {(c, k): [] for c in range(GR) for k in range(GC)}
    for i in range(GR):
        for cc in range(GC):
            for (g, off, w) in blocks(cc):
                d = (g - i) % GR
                if d in (DX1, DX2):
                    J[(i, cc)].append((i, g, off, w, cc, tuple(range(GC))))
                else:
                    for k in range(GC):
                        J[(i if d == 0 else (i - DW) % GR, k)].append((i, g, off, w, cc, (k,)))
    return J


def ops_for(c, k, J, L):
    ops = []
    for b, (i, gg, off, w, cc, kks) in enumerate(J):
        for kk in kks:
            col = xcol(c, k, gg, kk, cc)
            for t in range(KT):
                wc = ((WO if kk == k else WP) if i == c else WA) + NC * t
                xc = col + w * t
                hit = [l for l in L if l[0] in ("q", "p") and any(l[1] < a + NC and a < l[2] for a in (wc, xc))]
                ops.append((max([l[4] for l in hit] + [0]), int(i == c), b, kk, t, wc, xc, sorted(set(l[3] for l in hit))))
    ops.sort(key=lambda o: o[:5])
    return ops


def finish_order(ops):
    return [o[2] for n, o in enumerate(ops) if not any(p[2] == o[2] for p in ops[n + 1:])]


def bits(m):
    return [b for b in range(m.bit_length()) if (m >> b) & 1]


def lane(pool, n):
    return pool if n is None else pool[n * len(pool) // 2:(n + 1) * len(pool) // 2]


def plan_all(cores, topo):
    calls, lands, need, J = {}, {}, {}, jobs_all()

    def add(me, waits, pool, trs, est):
        for wd in sorted(set(t[2] for t in trs), reverse=True):
            grp = [t for t in trs if t[2] == wd]
            calls.setdefault(me, []).append((waits, pool, grp))
            waits = []
            for (buf, sc, nc, d, dc, sn) in grp:
                lands.setdefault(d, []).append((buf, dc, dc + nc, sn, est))
                need.setdefault(d, {})
                need[d][sn] = need[d].get(sn, 0) + len(pool) // len(grp)

    def floats(c, k, sel):
        w8, trs = [], []
        for b, (i, gg, off, w, cc, kks) in enumerate(J[(c, k)]):
            if (i, cc) != (c, k) and sel(i):
                w8.append("cp%d" % b)
                trs.append((("sb", "l%d" % k), NC * b, w, cores[i * GC + cc], NC * gg + off - CH * cc, "f%d" % blocks(cc).index((gg, off, w))))
        return w8, trs

    for s in range(N):
        g, k = divmod(s, GC)
        me, mate = cores[s], cores[g * GC + (1 - k)]
        up, mid = (g - DW) % GR, (g - DX1) % GR
        lo = bits(topo.mask(me, cores[up * GC + k]))
        hi = [b for b in bits(topo.mask(me, mate)) if b not in lo]
        S = seg_src(g, k)
        md, mc = cores[mid * GC + k], xcol(mid, k, g, k, S[0][0])
        ud = cores[up * GC + k]
        rc = [c for c in range(NSIM) if topo.mates(topo.chip(c), topo.chip(ud)) and topo.die(c) == topo.die(me)
              and topo.may_write(c, ud)][0]
        hc = [c for c in range(NSIM) if topo.chip(c) == topo.chip(me) and topo.die(c) == topo.die(me) and c not in cores
              and topo.may_write(c, rc)][0]

        def owner(a):
            (c, off, ws, sc) = [e for e in S if e[3] <= a < e[3] + KT * e[2]][0]
            return cores[up * GC + c], xcol(up, c, g, k, c) + a - sc

        def hand(buf, a, w, sn, ln):
            own, dc = owner(a)
            add(me, [], lane(hi, ln), [(buf, a, w, hc, a, sn)], 0)
            add(hc, [sn], lane(bits(topo.mask(hc, rc)), ln), [(buf, a, w, rc, a, sn)], 0)
            add(rc, [sn], lane(bits(topo.mask(rc, own)), ln), [(buf, a, w, own, dc, "la%d" % k)], 8)

        for j in range(4):
            add(me, ["qx%d" % j], lane(lo, j % 2), [("q", XO + 128 * j, 128, md, mc + 128 * j, "xa" if j < 2 else "xb")], 2 + j // 2)
            if j < 2:
                hand("q", XO + 128 * j, 128, "h%d" % j, j)
            if j == 1:
                hand("p", XO, 256, "hp0", None)
        add(me, [], lo, [("p", XO, 512, md, mc, "xa")], 2)

        def both(buf, a, w, sn, waits, est):
            add(me, waits, lo + hi, [(buf, WO + a, w, ud, WA + a, sn), (buf, WO + a, w, mate, WP + a, "aw")], est)

        for j in range(4):
            w8 = ["qw%d" % j]
            if j % 2:
                both("p", 128 * (j - 1), 256, "dp%d" % (j // 2), w8, 3.75 + 0.5 * j)
                w8 = []
            both("q", 128 * j, 128, "d%d" % j, w8, 4 + 0.5 * j)
        own, dc = owner(XO + 256)
        for buf in ("p", "q"):
            add(me, [], lo, [(buf, XO + 256, 256, own, dc, "lb%d" % k)], 9)
        w8, trs = floats(g, k, lambda i: i == g)
        if trs:
            add(me, w8, hi, trs, 0)
        b1 = (g + DX1) % GR
        for n, buf in enumerate(("q", "p")):
            tx = [(buf, xcol(g, k, b1, k, c), KT * w, mate, xcol(g, c, b1, k, c), "xr") for (c, off, w, sc) in seg_src(b1, k) if c != k]
            if tx:
                add(me, [] if n else ["xa", "xb"], hi, tx, 7)
        w8, trs = floats(g, k, lambda i: i != g)
        add(me, w8, lo, trs, 0)
    return calls, lands, need, J


def remote_calls(g, T, topo, calls, need):
    sem = T.sem
    sent = 0
    for (waits, pool, trs) in calls:
        for nm in waits:
            g.wait_ge(sem[nm], need.get(nm, 1))
        n = len(pool) // len(trs)
        out = []
        for j, (buf, sc, nc, d, dc, sn) in enumerate(trs):
            mask = sum(1 << b for b in pool[j * n:(j + 1) * n])
            if buf == "q":
                src, dst = T.q[:, sc:sc + nc].bitcast(dt.uint8), T.q[:, dc:dc + nc].bitcast(dt.uint8)
            elif buf == "p":
                src, dst = T.p[:, sc:sc + nc], T.p[:, dc:dc + nc]
            else:
                src, dst = T[buf[0]][:, sc:sc + nc], T[buf[1]][:, dc:dc + nc]
            rid, pid, _ = topo.addr(d)
            out.append((src, dst, rid, pid, mask, sem[sn]))
            sent += n
        if len(out) == 1:
            src, dst, rid, pid, mask, sn = out[0]
            g.remote_dma(out_ap=dst, in_ap=src, remote_sem=sn, local_sem=sem.sent, pid=pid, routing_id=rid, dma_engine_mask=mask)
        else:
            g.remote_dma_fused([RemoteDMATransfer(dst_ids=[DstId(rid=rid, pnc=pid)], dma_engine_mask=mask, remote_sem=sn, src=src, dst=dst)
                                for (src, dst, rid, pid, mask, sn) in out], local_sem=sem.sent)
    g.wait_ge(sem.sent, sent)


def rank_program(g, core, T, topo):
    cores = list(T.cores)
    if "plan" not in MEMO:
        MEMO["plan"] = plan_all(cores, topo)
    if core not in MEMO["plan"][0]:
        return
    calls, lands, need = (d[core] for d in MEMO["plan"][:3])
    r = T.rank_of(core)
    if r is None:
        remote_calls(g, T, topo, calls, need)
        return
    i, k = divmod(r, GC)
    J = MEMO["plan"][3][(i, k)]
    sem = T.sem

    dq = [g.sync, g.scalar]
    S = seg_src(i, k)
    for m in range(8):
        a = 256 * m if len(S) == 1 else 512 * (m % KT) + 4 * S[m // KT][1]
        dq[m % 2].dma_start(T.xb[:, 256 * m:256 * m + 256], T.x[:, a:a + 256]).then_inc(sem["lx%d" % (m // 2)], 16)
    for m in range(8):
        dq[m % 2].dma_start(T.wb[:, 256 * m:256 * m + 256], T.w[:, 256 * m:256 * m + 256]).then_inc(sem["lw%d" % (m // 2)], 16)

    v = g.vector
    for (nm, buf, col) in (("x", T.xb, XO), ("w", T.wb, WO)):
        for h in range(4):
            v.wait_ge(sem["l%s%d" % (nm, h)], 32)
            a = col + 128 * h
            v.quantize_mx(T.q[:, a:a + 128], T.p[:, a:a + 128], buf[:, 512 * h:512 * h + 512]).then_inc(sem["q%s%d" % (nm, h)], 1)

    remote_calls(g, T, topo, calls, need)

    made = [("q", c0 + 128 * j, c0 + 128 * j + 128, "q%s%d" % (nm, j), e0 + 0.2 * j) for (nm, c0, e0) in (("x", XO, 0), ("w", WO, 3)) for j in range(4)]
    ops = ops_for(i, k, J, lands + made)
    done = finish_order(ops)
    te = g.tensor
    seen = set()
    for n, (est, own, b, kk, t, wc, xc, deps) in enumerate(ops):
        for sn in deps:
            if sn not in seen:
                seen.add(sn)
                te.wait_ge(sem[sn], need.get(sn, 1))
        first = not any(o[2] == b for o in ops[:n])
        last = not any(o[2] == b for o in ops[n + 1:])
        ins = te.matmul_mx(T.ps[:, 512 * b:512 * b + NC], T.q[:, wc:wc + NC], T.p[:, wc:wc + NC],
                           T.q[:, xc:xc + NC], T.p[:, xc:xc + NC], first, last)
        if last:
            ins.then_inc(sem["mm%d" % b], 1)

    mine = blocks(k)
    stays = [b for b in done if (J[b][0], J[b][4]) == (i, k) and len(J[b][5]) < GC]
    seq = [b for b in done if b not in stays]
    at = [n for n, b in enumerate(seq) if (J[b][1] - i) % GR == DX2 and J[b][0] == i]
    at = at[0] if at else len(seq)
    ready = {}
    for b in seq[:at] + stays + seq[at:]:
        ii, gg, off, w, cc, kks = J[b]
        v.wait_ge(sem["mm%d" % b], 1)
        acc = T.ps[:, 512 * b:512 * b + w]
        if (ii, cc) != (i, k):
            ins = v.tensor_copy(T.sb[:, NC * b:NC * b + w], acc)
        else:
            y0 = NC * gg + off - CH * k
            ready[(gg, off, w)] = "cp%d" % b
            if b in stays:
                fs = "f%d" % mine.index((gg, off, w))
                v.wait_ge(sem[fs], need[fs])
                ins = v.tensor_tensor(T.ob[:, y0:y0 + w], acc, T["l%d" % (1 - k)][:, y0:y0 + w], AluOpType.add)
            else:
                ins = v.tensor_copy(T.ob[:, y0:y0 + w], acc)
        ins.then_inc(sem["cp%d" % b], 1)
    for bi, (gg, off, w) in enumerate(mine):
        if (gg, off, w) not in ready:
            y0 = NC * gg + off - CH * k
            v.wait_ge(sem["f%d" % bi], need["f%d" % bi])
            v.tensor_tensor(T.ob[:, y0:y0 + w], T.l0[:, y0:y0 + w], T.l1[:, y0:y0 + w], AluOpType.add).then_inc(sem["ad%d" % bi], 1)
            ready[(gg, off, w)] = "ad%d" % bi

    when = {DX1: 0, 0: 1, DX2: 2}
    todo = sorted(enumerate(mine), key=lambda e: when.get((e[1][0] - i) % GR, 3))
    for n, (bi, blk) in enumerate(todo):
        gg, off, w = blk
        y0 = NC * gg + off - CH * k
        d = dq[n % 2]
        d.wait_ge(sem[ready[blk]], 1)
        d.dma_start(T.y[:, y0:y0 + w], T.ob[:, y0:y0 + w]).then_inc(sem["st%d" % bi], 16)
    for n, (bi, blk) in enumerate(todo):
        dq[n % 2].wait_ge(sem["st%d" % bi], 16)
